import numpy as np
import ml_dtypes


def mxq(x, axis, fmt="e4m3"):
    dtype, down = {"e4m3": (ml_dtypes.float8_e4m3fn, 7), "e5m2": (ml_dtypes.float8_e5m2, 14)}[fmt]
    v = np.moveaxis(np.asarray(x, np.float32).astype(ml_dtypes.bfloat16).astype(np.float64), axis, -1)
    blocks = v.reshape(v.shape[:-1] + (-1, 32))
    amax = np.abs(blocks).max(-1, keepdims=True)
    byte = np.maximum(np.where(amax > 0, np.frexp(amax)[1] - 1 + 127, 0) - down, 1)
    scale = np.exp2(byte - 127.0)
    codes = (blocks / scale).astype(np.float32).astype(dtype).astype(np.float64)
    return np.moveaxis((codes * scale).reshape(v.shape), -1, axis)


WIDE = False


def mx_kscale(k):
    if not WIDE:
        return np.ones(k)
    levels = np.array([10, -10, 5, -5, 0])
    if k % 512:
        return np.exp2(np.random.permutation(np.resize(levels, k // 32))).repeat(32)
    a = np.empty((k // 512, 16))
    for p in range(k // 512):
        a[p, :8] = np.random.permutation(np.resize(levels, 8))
        for g in range(8):
            far = levels[np.abs(levels - a[p, g]) >= 10]
            a[p, g + 8] = far[np.random.randint(len(far))]
    return np.exp2(a.ravel()).repeat(32)


def f64(x):
    return np.asarray(x).astype(np.float64)


def striped(idx):
    return np.tile(idx.reshape(-1, 16).T, (8, 1)).astype(np.uint16)


def unstriped(offs):
    return offs[:16].T.reshape(-1).astype(np.int64)


def silu(v):
    return v / (1.0 + np.exp(-np.maximum(v, -700.0)))


K, T, E, C, H, N = 512, 512, 8, 128, 512, 128


def by_expert(wq, xq):
    return np.concatenate([wq[e].T @ xq[:, e * C:(e + 1) * C] for e in range(E)], axis=1)


def setup_inputs():
    n = np.random.standard_normal
    s = mx_kscale(K)[:, None]
    u = mx_kscale(H)
    first = np.random.permutation(np.repeat(np.arange(E), T // E))
    second = (first + 1 + np.random.permutation(np.repeat(np.arange(E - 1), -(-T // (E - 1)))[:T])) % E
    while np.bincount(second, minlength=E).max() != T // E:
        load = np.bincount(second, minlength=E); hi, lo = int(load.argmax()), int(load.argmin())
        t = np.flatnonzero((second == hi) & (first != lo))[0]; second[t] = lo
    slot_token = np.empty(E * C, np.int64); pos = np.empty((2, T), np.int64); fill = np.zeros(E, np.int64)
    place = np.stack([np.random.permutation(C) for _ in range(E)])
    for r, deal in enumerate((first, second)):
        for t in np.random.permutation(T):
            e = deal[t]; j = e * C + place[e, fill[e]]; fill[e] += 1; slot_token[j] = t; pos[r, t] = j
    g = np.random.uniform(0.2, 0.8, T)
    return {
        "xT": (n((K, T)) * s).astype(np.float32),
        "w1": (n((E, K, H)) / np.sqrt(K) / s[None]).astype(np.float32),
        "w3": (n((E, K, H)) / np.sqrt(K) / s[None] * u[None, None, :]).astype(np.float32),
        "w2": (n((E, H, N)) / np.sqrt(H) / u[None, :, None]).astype(np.float32),
        "gate": np.stack([np.tile(g, (N, 1)), np.tile(1.0 - g, (N, 1))]).astype(np.float32),
        "offs": striped(slot_token),
        "pos1": striped(pos[0]),
        "pos2": striped(pos[1]),
    }


def reference(xT, w1, w3, w2, gate, offs, pos1, pos2):
    idx = unstriped(offs)
    xq = mxq(f64(xT)[:, idx], 0, "e4m3")
    h = silu(by_expert(mxq(f64(w1), 1, "e4m3"), xq))
    h = h * by_expert(mxq(f64(w3), 1, "e4m3"), xq)
    y = by_expert(mxq(f64(w2), 1, "e4m3"), mxq(h, 0, "e4m3"))
    return f64(gate[0]) * y[:, unstriped(pos1)] + f64(gate[1]) * y[:, unstriped(pos2)]

@@ -1,0 +1,163 @@
+from contextlib import ExitStack
+
+import concourse.mybir as mybir
+
+K, T, E, C, H, N = 512, 512, 8, 128, 512, 128
+SLOTS = E * C
+FLOPS = 2 * SLOTS * (2 * K * H + H * N)
+
+F32 = mybir.dt.float32
+BF16 = mybir.dt.bfloat16
+U32 = mybir.dt.uint32
+U16 = mybir.dt.uint16
+U8 = mybir.dt.uint8
+FP8X4 = mybir.dt.float8_e4m3fn_x4
+MULT = mybir.AluOpType.mult
+ADD = mybir.AluOpType.add
+SILU = mybir.ActivationFunctionType.Silu
+
+P = 128
+J = 4
+PIECE = 256
+
+
+def tile_routed_moe_kernel(tc, xT, w1, w3, w2, gate, offs, pos1, pos2, out):
+    nc = tc.nc
+    with ExitStack() as ctx:
+        held = ctx.enter_context(tc.tile_pool(name="held", bufs=1))
+        stage = ctx.enter_context(tc.tile_pool(name="stage", bufs=2))
+        psum = ctx.enter_context(tc.psum_pool(name="psum", bufs=3))
+
+        offs_t = held.tile([P, SLOTS // 16], U16, name="offs_t")
+        pos1_t = held.tile([P, T // 16], U16, name="pos1_t")
+        pos2_t = held.tile([P, T // 16], U16, name="pos2_t")
+        x_raw = held.tile([P, J * T], F32, name="x_raw")
+        gates = held.tile([P, 2, T], F32, name="gates")
+        w1_raw = [held.tile([P, J * H], F32, name=f"w1_raw{e}") for e in range(E)]
+        w3_raw = [held.tile([P, J * H], F32, name=f"w3_raw{e}") for e in range(E)]
+        w2_raw = [held.tile([P, J * N], F32, name=f"w2_raw{e}") for e in range(E)]
+
+        def load_up(raw, w, e):
+            nc.sync.dma_start(out=raw[e][:], in_=w[e, :, :].rearrange("(p j) h -> p (j h)", j=J))
+
+        nc.sync.dma_start(offs_t[:], offs)
+        nc.sync.dma_start(out=x_raw[:], in_=xT.rearrange("(p j) t -> p (j t)", j=J))
+        for e in range(E):
+            load_up(w1_raw, w1, e)
+            if e < E - 1:
+                load_up(w3_raw, w3, e)
+            else:
+                half_dst = w3_raw[e][:].rearrange("p (j h) -> p j h", j=J)
+                half_src = w3[e, :, :].rearrange("(p j) h -> p j h", j=J)
+                for s in (slice(0, H // 2), slice(H // 2, H)):
+                    nc.sync.dma_start(out=half_dst[:, :, s], in_=half_src[:, :, s])
+            if e == 0:
+                nc.sync.dma_start(pos1_t[:], pos1)
+                nc.sync.dma_start(pos2_t[:], pos2)
+            if e < E - 2:
+                load_up(w2_raw, w2, e)
+        load_up(w2_raw, w2, E - 2)
+        load_up(w2_raw, w2, E - 1)
+        for g in range(2):
+            nc.sync.dma_start(out=gates[:, g, :], in_=gate[g, :, :])
+
+        warm = held.tile([P, 1], F32, name="warm")
+        nc.vector.memset(warm[:], 0.0)
+        nc.scalar.activation(warm[:], warm[:], SILU)
+
+        x_codes = held.tile([P, T], U32, name="x_codes", align_bytes=64)
+        x_scales = held.tile([P, T], U8, name="x_scales", align_bytes=64)
+        nc.gpsimd.memset(x_scales[:], 0)
+        x_grouped = held.tile([P, T * J], BF16, name="x_grouped", align_bytes=64)
+        x_src = x_raw[:].rearrange("p (j c i) -> p c j i", j=J, i=4)
+        x_dst = x_grouped[:].rearrange("p (c i j) -> p c j i", i=4, j=J)
+        nc.vector.tensor_copy(out=x_dst[:, 0:64], in_=x_src[:, 0:64])
+        nc.scalar.copy(out=x_dst[:, 64:128], in_=x_src[:, 64:128])
+        nc.vector.quantize_mx(out=x_codes[:].bitcast(FP8X4), scales=x_scales[:], in_=x_grouped[:])
+
+        s_codes = held.tile([P, SLOTS], U32, name="s_codes", align_bytes=64)
+        s_scales = held.tile([P, SLOTS], U8, name="s_scales", align_bytes=64)
+
+        def gather(g):
+            cols = slice(g * PIECE, (g + 1) * PIECE)
+            lst = offs_t[:, g * (PIECE // 16):(g + 1) * (PIECE // 16)]
+            nc.vector.tensor_copy(s_codes[:, cols], x_codes[:].indirect(lst))
+            nc.vector.tensor_copy(s_scales[:, cols], x_scales[:].indirect(lst))
+
+        y_sb = held.tile([P, SLOTS], F32, name="y_sb")
+
+        def up_views(raw, grouped):
+            src = raw[:].rearrange("p (j m t) -> p m j t", j=J, t=4)
+            dst = grouped[:].rearrange("p (t m j) -> p m j t", t=4, j=J)
+            return src, dst
+
+        for e in range(E):
+            if e % 2 == 0:
+                gather(e // 2)
+            cols = slice(e * C, (e + 1) * C)
+            last = e == E - 1
+
+            g1 = stage.tile([P, H * J], BF16, name="g1", align_bytes=64)
+            g3 = stage.tile([P, H * J], BF16, name="g3", align_bytes=64)
+            src, dst = up_views(w1_raw[e], g1)
+            nc.scalar.copy(out=dst, in_=src)
+            q1 = stage.tile([P, H], U32, name="q1", align_bytes=64)
+            s1 = stage.tile([P, H], U8, name="s1", align_bytes=64)
+            nc.vector.quantize_mx(out=q1[:].bitcast(FP8X4), scales=s1[:], in_=g1[:])
+
+            acc_a = psum.tile([P, 4, C], F32, name="acc_a", bufs=3)
+            for t in range(4):
+                nc.tensor.matmul_mx(
+                    out=acc_a[:, t, :], lhsT=q1[:, t * P:(t + 1) * P].bitcast(FP8X4),
+                    lhsT_scale=s1[:, t * P:(t + 1) * P], rhs=s_codes[:, cols].bitcast(FP8X4),
+                    rhs_scale=s_scales[:, cols], start=True, stop=True)
+            sil = stage.tile([P, C, 4], F32, name="sil")
+            nc.scalar.activation(sil[:], acc_a[:].rearrange("p t c -> p c t"), SILU)
+
+            src, dst = up_views(w3_raw[e], g3)
+            if not last:
+                nc.vector.tensor_copy(out=dst, in_=src)
+            else:
+                for m0 in (0, 64):
+                    nc.vector.tensor_copy(out=dst[:, m0:m0 + 40], in_=src[:, m0:m0 + 40])
+                    nc.scalar.copy(out=dst[:, m0 + 40:m0 + 64], in_=src[:, m0 + 40:m0 + 64])
+            q3 = stage.tile([P, H], U32, name="q3", align_bytes=64)
+            s3 = stage.tile([P, H], U8, name="s3", align_bytes=64)
+            nc.vector.quantize_mx(out=q3[:].bitcast(FP8X4), scales=s3[:], in_=g3[:])
+            acc_b = psum.tile([P, 4, C], F32, name="acc_b", bufs=3)
+            for t in range(4):
+                nc.tensor.matmul_mx(
+                    out=acc_b[:, t, :], lhsT=q3[:, t * P:(t + 1) * P].bitcast(FP8X4),
+                    lhsT_scale=s3[:, t * P:(t + 1) * P], rhs=s_codes[:, cols].bitcast(FP8X4),
+                    rhs_scale=s_scales[:, cols], start=True, stop=True)
+
+            g2 = stage.tile([P, N * J], BF16, name="g2", align_bytes=64)
+            nc.scalar.copy(
+                out=g2[:].rearrange("p (c i j) -> p c j i", i=4, j=J),
+                in_=w2_raw[e][:].rearrange("p (j c i) -> p c j i", j=J, i=4))
+            q2 = stage.tile([P, N], U32, name="q2", align_bytes=64)
+            s2 = stage.tile([P, N], U8, name="s2", align_bytes=64)
+            nc.vector.quantize_mx(out=q2[:].bitcast(FP8X4), scales=s2[:], in_=g2[:])
+
+            hb = stage.tile([P, C, 4], BF16, name="hb", align_bytes=64)
+            nc.vector.tensor_tensor(hb[:], acc_b[:].rearrange("p t c -> p c t"), sil[:], MULT)
+            qh = stage.tile([P, C], U32, name="qh", align_bytes=64)
+            sh = stage.tile([P, C], U8, name="sh", align_bytes=64)
+            nc.vector.quantize_mx(out=qh[:].bitcast(FP8X4), scales=sh[:], in_=hb[:].rearrange("p c t -> p (c t)"))
+
+            acc_y = psum.tile([P, C], F32, name="acc_y", bufs=2)
+            nc.tensor.matmul_mx(
+                out=acc_y[:], lhsT=q2[:].bitcast(FP8X4), lhsT_scale=s2[:],
+                rhs=qh[:].bitcast(FP8X4), rhs_scale=sh[:], start=True, stop=True)
+            nc.scalar.copy(out=y_sb[:, cols], in_=acc_y[:])
+
+        for h in range(2):
+            toks = slice(h * 256, (h + 1) * 256)
+            lst = slice(h * 16, (h + 1) * 16)
+            r1 = stage.tile([P, 256], F32, name="r1")
+            r2 = stage.tile([P, 256], F32, name="r2")
+            nc.vector.tensor_tensor(r1[:], y_sb[:].indirect(pos1_t[:, lst]), gates[:, 0, toks], MULT)
+            nc.vector.tensor_tensor(r2[:], y_sb[:].indirect(pos2_t[:, lst]), gates[:, 1, toks], MULT)
+            res = stage.tile([P, 256], F32, name="res")
+            nc.vector.tensor_tensor(res[:], r1[:], r2[:], ADD)
+            nc.sync.dma_start(out=out[:, toks], in_=res[:])

@@ -18,7 +18,17 @@ SILU = mybir.ActivationFunctionType.Silu
 
 P = 128
 J = 4
-PIECE = 256
+LOADS = "offs xa xb w10 w30 w11 w31 w20 pos w12 w32 w13 w33 w14 w34 w15 w35 w24 w16 w36 w17 w37a w37b w26 g0 g1".split()
+GATHERS = ((0, 2), (2, 3), (5, 3))
+GATHER_AT = {0: 0, 1: 1, 3: 2}
+Y_GROUPS = ((0, 1, 2, 3), (4, 5, 6), (7,))
+W2_GROUPS = ((0, 1, 2, 3), (4, 5), (6, 7))
+W2_AT = {1: (0, 1, 2, 3), 5: (4, 5), 7: (6, 7)}
+W2_ON_VECTOR = ()
+V1 = {7: 64}
+S3 = {7: (24, 24)}
+SEPARATE = (7,)
+XV = (256, 256)
 
 
 def tile_routed_moe_kernel(tc, xT, w1, w3, w2, gate, offs, pos1, pos2, out):
@@ -31,133 +41,193 @@ def tile_routed_moe_kernel(tc, xT, w1, w3, w2, gate, offs, pos1, pos2, out):
         offs_t = held.tile([P, SLOTS // 16], U16, name="offs_t")
         pos1_t = held.tile([P, T // 16], U16, name="pos1_t")
         pos2_t = held.tile([P, T // 16], U16, name="pos2_t")
-        x_raw = held.tile([P, J * T], F32, name="x_raw")
-        gates = held.tile([P, 2, T], F32, name="gates")
+        x_raw = [held.tile([P, J, T // 2], F32, name=f"x_raw{h}") for h in range(2)]
+        gates = [held.tile([P, T], F32, name=f"gates{g}") for g in range(2)]
         w1_raw = [held.tile([P, J * H], F32, name=f"w1_raw{e}") for e in range(E)]
         w3_raw = [held.tile([P, J * H], F32, name=f"w3_raw{e}") for e in range(E)]
-        w2_raw = [held.tile([P, J * N], F32, name=f"w2_raw{e}") for e in range(E)]
-
-        def load_up(raw, w, e):
-            nc.sync.dma_start(out=raw[e][:], in_=w[e, :, :].rearrange("(p j) h -> p (j h)", j=J))
-
-        nc.sync.dma_start(offs_t[:], offs)
-        nc.sync.dma_start(out=x_raw[:], in_=xT.rearrange("(p j) t -> p (j t)", j=J))
-        for e in range(E):
-            load_up(w1_raw, w1, e)
-            if e < E - 1:
-                load_up(w3_raw, w3, e)
-            else:
-                half_dst = w3_raw[e][:].rearrange("p (j h) -> p j h", j=J)
-                half_src = w3[e, :, :].rearrange("(p j) h -> p j h", j=J)
-                for s in (slice(0, H // 2), slice(H // 2, H)):
-                    nc.sync.dma_start(out=half_dst[:, :, s], in_=half_src[:, :, s])
-            if e == 0:
-                nc.sync.dma_start(pos1_t[:], pos1)
-                nc.sync.dma_start(pos2_t[:], pos2)
-            if e < E - 2:
-                load_up(w2_raw, w2, e)
-        load_up(w2_raw, w2, E - 2)
-        load_up(w2_raw, w2, E - 1)
-        for g in range(2):
-            nc.sync.dma_start(out=gates[:, g, :], in_=gate[g, :, :])
+        w2_raw = {g: held.tile([P, len(g), J * N], F32, name=f"w2_raw{g[0]}") for g in W2_GROUPS}
 
         warm = held.tile([P, 1], F32, name="warm")
         nc.vector.memset(warm[:], 0.0)
         nc.scalar.activation(warm[:], warm[:], SILU)
 
+        for name in LOADS:
+            if name == "offs":
+                nc.sync.dma_start(offs_t[:], offs)
+            elif name == "pos":
+                nc.sync.dma_start(pos1_t[:], pos1)
+                nc.sync.dma_start(pos2_t[:], pos2)
+            elif name[0] == "x":
+                h = "ab".index(name[1])
+                nc.sync.dma_start(out=x_raw[h][:], in_=xT[:, h * (T // 2):(h + 1) * (T // 2)].rearrange("(p j) t -> p j t", j=J))
+            elif name[0] == "g":
+                g = int(name[1])
+                nc.sync.dma_start(out=gates[g][:], in_=gate[g, :, :])
+            elif name[:2] == "w2":
+                for g in W2_GROUPS:
+                    if g[0] == int(name[2]):
+                        nc.sync.dma_start(out=w2_raw[g][:], in_=w2[g[0]:g[-1] + 1, :, :].rearrange("e (p j) n -> p e (j n)", j=J))
+            else:
+                e = int(name[2])
+                raw, w = (w1_raw[e], w1) if name[1] == "1" else (w3_raw[e], w3)
+                if len(name) == 3:
+                    nc.sync.dma_start(out=raw[:], in_=w[e, :, :].rearrange("(p j) h -> p (j h)", j=J))
+                else:
+                    a = "ab".index(name[3])
+                    s = slice(a * (H // 2), (a + 1) * (H // 2))
+                    nc.sync.dma_start(out=raw[:].rearrange("p (j h) -> p j h", j=J)[:, :, s],
+                                      in_=w[e, :, :].rearrange("(p j) h -> p j h", j=J)[:, :, s])
+
         x_codes = held.tile([P, T], U32, name="x_codes", align_bytes=64)
         x_scales = held.tile([P, T], U8, name="x_scales", align_bytes=64)
         nc.gpsimd.memset(x_scales[:], 0)
         x_grouped = held.tile([P, T * J], BF16, name="x_grouped", align_bytes=64)
-        x_src = x_raw[:].rearrange("p (j c i) -> p c j i", j=J, i=4)
-        x_dst = x_grouped[:].rearrange("p (c i j) -> p c j i", i=4, j=J)
-        nc.vector.tensor_copy(out=x_dst[:, 0:64], in_=x_src[:, 0:64])
-        nc.scalar.copy(out=x_dst[:, 64:128], in_=x_src[:, 64:128])
+        for h in range(2):
+            x_src = x_raw[h][:].rearrange("p j (c i) -> p c j i", i=4)
+            x_dst = x_grouped[:, h * 1024:(h + 1) * 1024].rearrange("p (c i j) -> p c j i", i=4, j=J)
+            cut = XV[h] // 4
+            if cut:
+                nc.vector.tensor_copy(out=x_dst[:, 0:cut], in_=x_src[:, 0:cut])
+            if cut < 64:
+                nc.scalar.copy(out=x_dst[:, cut:64], in_=x_src[:, cut:64])
         nc.vector.quantize_mx(out=x_codes[:].bitcast(FP8X4), scales=x_scales[:], in_=x_grouped[:])
 
         s_codes = held.tile([P, SLOTS], U32, name="s_codes", align_bytes=64)
         s_scales = held.tile([P, SLOTS], U8, name="s_scales", align_bytes=64)
+        y_sb = held.tile([P, SLOTS], F32, name="y_sb")
+        live = {}
 
-        def gather(g):
-            cols = slice(g * PIECE, (g + 1) * PIECE)
-            lst = offs_t[:, g * (PIECE // 16):(g + 1) * (PIECE // 16)]
+        def gather(first, count):
+            cols = slice(first * C, (first + count) * C)
+            lst = offs_t[:, first * C // 16:(first + count) * C // 16]
             nc.vector.tensor_copy(s_codes[:, cols], x_codes[:].indirect(lst))
             nc.vector.tensor_copy(s_scales[:, cols], x_scales[:].indirect(lst))
 
-        y_sb = held.tile([P, SLOTS], F32, name="y_sb")
-
-        def up_views(raw, grouped):
+        def up_views(raw, grouped, m0, m1):
             src = raw[:].rearrange("p (j m t) -> p m j t", j=J, t=4)
-            dst = grouped[:].rearrange("p (t m j) -> p m j t", t=4, j=J)
-            return src, dst
+            dst = grouped.rearrange("p (t m j) -> p m j t", t=4, j=J)
+            return src[:, m0:m1], dst[:, m0:m1]
 
-        for e in range(E):
-            if e % 2 == 0:
-                gather(e // 2)
+        def inter(which, e):
+            if which == 0:
+                live["g", e] = stage.tile([P, 2, H * J], BF16, name="grouped", align_bytes=64)
+            raw = (w1_raw, w3_raw)[which][e]
+            if which == 1 and e in S3:
+                parts = [(0, 64 - S3[e][0], 64), (64, 128 - S3[e][1], 128)]
+            else:
+                v = V1.get(e, 0) if which == 0 else 128
+                parts = [(0, v, 128)]
+            for lo, cut, hi in parts:
+                if hi > cut:
+                    src, dst = up_views(raw, live["g", e][:, which, :], cut, hi)
+                    nc.scalar.copy(out=dst, in_=src)
+                if cut > lo:
+                    src, dst = up_views(raw, live["g", e][:, which, :], lo, cut)
+                    nc.vector.tensor_copy(out=dst, in_=src)
+
+        def products(which, e):
+            codes, scales = live["q", e]
+            acc = psum.tile([P, 4, C], F32, name=f"acc{which}", bufs=3)
             cols = slice(e * C, (e + 1) * C)
-            last = e == E - 1
-
-            g1 = stage.tile([P, H * J], BF16, name="g1", align_bytes=64)
-            g3 = stage.tile([P, H * J], BF16, name="g3", align_bytes=64)
-            src, dst = up_views(w1_raw[e], g1)
-            nc.scalar.copy(out=dst, in_=src)
-            q1 = stage.tile([P, H], U32, name="q1", align_bytes=64)
-            s1 = stage.tile([P, H], U8, name="s1", align_bytes=64)
-            nc.vector.quantize_mx(out=q1[:].bitcast(FP8X4), scales=s1[:], in_=g1[:])
-
-            acc_a = psum.tile([P, 4, C], F32, name="acc_a", bufs=3)
             for t in range(4):
+                blk = slice(which * H + t * P, which * H + (t + 1) * P)
                 nc.tensor.matmul_mx(
-                    out=acc_a[:, t, :], lhsT=q1[:, t * P:(t + 1) * P].bitcast(FP8X4),
-                    lhsT_scale=s1[:, t * P:(t + 1) * P], rhs=s_codes[:, cols].bitcast(FP8X4),
-                    rhs_scale=s_scales[:, cols], start=True, stop=True)
-            sil = stage.tile([P, C, 4], F32, name="sil")
-            nc.scalar.activation(sil[:], acc_a[:].rearrange("p t c -> p c t"), SILU)
+                    out=acc[:, t, :], lhsT=codes[:, blk].bitcast(FP8X4), lhsT_scale=scales[:, blk],
+                    rhs=s_codes[:, cols].bitcast(FP8X4), rhs_scale=s_scales[:, cols], start=True, stop=True)
+            live["acc", which, e] = acc
 
-            src, dst = up_views(w3_raw[e], g3)
-            if not last:
+        def quant(whichs, e):
+            if whichs[0] == 0:
+                codes = stage.tile([P, 2 * H], U32, name="codes", align_bytes=64)
+                scales = stage.tile([P, 2 * H], U8, name="scales", align_bytes=64)
+                live["q", e] = codes, scales
+            codes, scales = live["q", e]
+            cols = slice(whichs[0] * H, (whichs[-1] + 1) * H)
+            words = slice(whichs[0] * H * J, (whichs[-1] + 1) * H * J)
+            nc.vector.quantize_mx(out=codes[:, cols].bitcast(FP8X4), scales=scales[:, cols],
+                                  in_=live["g", e][:].rearrange("p w k -> p (w k)")[:, words])
+            for which in whichs:
+                products(which, e)
+
+        def silu(e):
+            sil = stage.tile([P, C, 4], F32, name="sil")
+            nc.scalar.activation(sil[:], live["acc", 0, e][:].rearrange("p t c -> p c t"), SILU)
+            live["sil", e] = sil
+
+        def inter2(g):
+            grouped = held.tile([P, len(g), N * J], BF16, name=f"grp2_{g[0]}", align_bytes=64)
+            src = w2_raw[g][:].rearrange("p e (j c i) -> p e c j i", j=J, i=4)
+            dst = grouped[:].rearrange("p e (c i j) -> p e c j i", i=4, j=J)
+            if g in W2_ON_VECTOR:
                 nc.vector.tensor_copy(out=dst, in_=src)
             else:
-                for m0 in (0, 64):
-                    nc.vector.tensor_copy(out=dst[:, m0:m0 + 40], in_=src[:, m0:m0 + 40])
-                    nc.scalar.copy(out=dst[:, m0 + 40:m0 + 64], in_=src[:, m0 + 40:m0 + 64])
-            q3 = stage.tile([P, H], U32, name="q3", align_bytes=64)
-            s3 = stage.tile([P, H], U8, name="s3", align_bytes=64)
-            nc.vector.quantize_mx(out=q3[:].bitcast(FP8X4), scales=s3[:], in_=g3[:])
-            acc_b = psum.tile([P, 4, C], F32, name="acc_b", bufs=3)
-            for t in range(4):
-                nc.tensor.matmul_mx(
-                    out=acc_b[:, t, :], lhsT=q3[:, t * P:(t + 1) * P].bitcast(FP8X4),
-                    lhsT_scale=s3[:, t * P:(t + 1) * P], rhs=s_codes[:, cols].bitcast(FP8X4),
-                    rhs_scale=s_scales[:, cols], start=True, stop=True)
+                nc.scalar.copy(out=dst, in_=src)
+            codes = held.tile([P, len(g), N], U32, name=f"cod2_{g[0]}", align_bytes=64)
+            scales = held.tile([P, len(g), N], U8, name=f"scl2_{g[0]}", align_bytes=64)
+            nc.vector.quantize_mx(
+                out=codes[:].rearrange("p e n -> p (e n)").bitcast(FP8X4),
+                scales=scales[:].rearrange("p e n -> p (e n)"), in_=grouped[:].rearrange("p e n -> p (e n)"))
+            for i, e in enumerate(g):
+                live["w2", e] = codes[:, i, :], scales[:, i, :]
 
-            g2 = stage.tile([P, N * J], BF16, name="g2", align_bytes=64)
-            nc.scalar.copy(
-                out=g2[:].rearrange("p (c i j) -> p c j i", i=4, j=J),
-                in_=w2_raw[e][:].rearrange("p (j c i) -> p c j i", j=J, i=4))
-            q2 = stage.tile([P, N], U32, name="q2", align_bytes=64)
-            s2 = stage.tile([P, N], U8, name="s2", align_bytes=64)
-            nc.vector.quantize_mx(out=q2[:].bitcast(FP8X4), scales=s2[:], in_=g2[:])
+        group_of = {e: g for g in Y_GROUPS for e in g}
 
+        def hid(e):
             hb = stage.tile([P, C, 4], BF16, name="hb", align_bytes=64)
-            nc.vector.tensor_tensor(hb[:], acc_b[:].rearrange("p t c -> p c t"), sil[:], MULT)
-            qh = stage.tile([P, C], U32, name="qh", align_bytes=64)
-            sh = stage.tile([P, C], U8, name="sh", align_bytes=64)
-            nc.vector.quantize_mx(out=qh[:].bitcast(FP8X4), scales=sh[:], in_=hb[:].rearrange("p c t -> p (c t)"))
+            nc.vector.tensor_tensor(hb[:], live["acc", 1, e][:].rearrange("p t c -> p c t"), live["sil", e][:], MULT)
+            live["hb", e] = hb
 
-            acc_y = psum.tile([P, C], F32, name="acc_y", bufs=2)
+        def quanth(e):
+            codes = stage.tile([P, C], U32, name="codh", align_bytes=64)
+            scales = stage.tile([P, C], U8, name="sclh", align_bytes=64)
+            nc.vector.quantize_mx(out=codes[:].bitcast(FP8X4), scales=scales[:],
+                                  in_=live["hb", e][:].rearrange("p c t -> p (c t)"))
+            grp = group_of[e]
+            if e == grp[0]:
+                live["y", grp] = psum.tile([P, 4, C], F32, name="acc_y", bufs=2)
+            w2c, w2s = live["w2", e]
             nc.tensor.matmul_mx(
-                out=acc_y[:], lhsT=q2[:].bitcast(FP8X4), lhsT_scale=s2[:],
-                rhs=qh[:].bitcast(FP8X4), rhs_scale=sh[:], start=True, stop=True)
-            nc.scalar.copy(out=y_sb[:, cols], in_=acc_y[:])
+                out=live["y", grp][:, e - grp[0], :], lhsT=w2c.bitcast(FP8X4), lhsT_scale=w2s,
+                rhs=codes[:].bitcast(FP8X4), rhs_scale=scales[:], start=True, stop=True)
 
-        for h in range(2):
-            toks = slice(h * 256, (h + 1) * 256)
-            lst = slice(h * 16, (h + 1) * 16)
-            r1 = stage.tile([P, 256], F32, name="r1")
-            r2 = stage.tile([P, 256], F32, name="r2")
-            nc.vector.tensor_tensor(r1[:], y_sb[:].indirect(pos1_t[:, lst]), gates[:, 0, toks], MULT)
-            nc.vector.tensor_tensor(r2[:], y_sb[:].indirect(pos2_t[:, lst]), gates[:, 1, toks], MULT)
-            res = stage.tile([P, 256], F32, name="res")
-            nc.vector.tensor_tensor(res[:], r1[:], r2[:], ADD)
-            nc.sync.dma_start(out=out[:, toks], in_=res[:])
+        def fetch(grp):
+            nc.scalar.copy(
+                out=y_sb[:, grp[0] * C:(grp[-1] + 1) * C].rearrange("p (g c) -> p g c", c=C),
+                in_=live["y", grp][:, 0:len(grp), :])
+
+        for e in range(E + 1):
+            if e in GATHER_AT:
+                gather(*GATHERS[GATHER_AT[e]])
+            if e < E:
+                inter(0, e)
+                if e in SEPARATE:
+                    quant((0,), e)
+                    silu(e)
+                    if e > 0:
+                        hid(e - 1)
+                inter(1, e)
+            if 0 < e < E and e not in SEPARATE:
+                hid(e - 1)
+            if e < E:
+                if e in SEPARATE:
+                    quant((1,), e)
+                else:
+                    quant((0, 1), e)
+                    silu(e)
+            if e in W2_AT:
+                inter2(W2_AT[e])
+            if e == E:
+                hid(e - 1)
+            if e > 0:
+                quanth(e - 1)
+                if e - 1 == group_of[e - 1][-1]:
+                    fetch(group_of[e - 1])
+
+        r1 = held.tile([P, T], F32, name="r1")
+        r2 = held.tile([P, T], F32, name="r2")
+        nc.vector.tensor_tensor(r1[:], y_sb[:].indirect(pos1_t[:]), gates[0][:], MULT)
+        nc.vector.tensor_tensor(r2[:], y_sb[:].indirect(pos2_t[:]), gates[1][:], MULT)
+        res = held.tile([P, T], F32, name="res")
+        for queue, toks in ((nc.sync, slice(0, T // 2)), (nc.scalar, slice(T // 2, T))):
+            nc.vector.tensor_tensor(res[:, toks], r1[:, toks], r2[:, toks], ADD)
+            queue.dma_start(out=out[:, toks], in_=res[:, toks])

@@ -18,15 +18,15 @@ SILU = mybir.ActivationFunctionType.Silu
 
 P = 128
 J = 4
-LOADS = "offs xa xb w10 w30 w11 w31 w20 pos w12 w32 w13 w33 w14 w34 w15 w35 w24 w16 w36 w17 w37a w37b w26 g0 g1".split()
+LOADS = "offs xa xb w10 w30 w11 w31 pos w12 w32 w13 w33 w14 w34 w15 w35 w16 w36 w17 w37 w20 w24 w26 gate".split()
 GATHERS = ((0, 2), (2, 3), (5, 3))
 GATHER_AT = {0: 0, 1: 1, 3: 2}
-Y_GROUPS = ((0, 1, 2, 3), (4, 5, 6), (7,))
+Y_GROUPS = ((0, 1, 2, 3), (4, 5), (6, 7))
 W2_GROUPS = ((0, 1, 2, 3), (4, 5), (6, 7))
-W2_AT = {1: (0, 1, 2, 3), 5: (4, 5), 7: (6, 7)}
-W2_ON_VECTOR = ()
+W2_AT = {8: ((0, 1, 2, 3), (4, 5), (6, 7))}
+W2_ON_VECTOR = (3, 5, 6, 7)
 V1 = {7: 64}
-S3 = {7: (24, 24)}
+S3 = {7: 48}
 SEPARATE = (7,)
 XV = (256, 256)
 
@@ -42,7 +42,7 @@ def tile_routed_moe_kernel(tc, xT, w1, w3, w2, gate, offs, pos1, pos2, out):
         pos1_t = held.tile([P, T // 16], U16, name="pos1_t")
         pos2_t = held.tile([P, T // 16], U16, name="pos2_t")
         x_raw = [held.tile([P, J, T // 2], F32, name=f"x_raw{h}") for h in range(2)]
-        gates = [held.tile([P, T], F32, name=f"gates{g}") for g in range(2)]
+        gates = held.tile([P, 2, T], F32, name="gates")
         w1_raw = [held.tile([P, J * H], F32, name=f"w1_raw{e}") for e in range(E)]
         w3_raw = [held.tile([P, J * H], F32, name=f"w3_raw{e}") for e in range(E)]
         w2_raw = {g: held.tile([P, len(g), J * N], F32, name=f"w2_raw{g[0]}") for g in W2_GROUPS}
@@ -60,9 +60,8 @@ def tile_routed_moe_kernel(tc, xT, w1, w3, w2, gate, offs, pos1, pos2, out):
             elif name[0] == "x":
                 h = "ab".index(name[1])
                 nc.sync.dma_start(out=x_raw[h][:], in_=xT[:, h * (T // 2):(h + 1) * (T // 2)].rearrange("(p j) t -> p j t", j=J))
-            elif name[0] == "g":
-                g = int(name[1])
-                nc.sync.dma_start(out=gates[g][:], in_=gate[g, :, :])
+            elif name == "gate":
+                nc.sync.dma_start(out=gates[:], in_=gate.rearrange("g p t -> p g t"))
             elif name[:2] == "w2":
                 for g in W2_GROUPS:
                     if g[0] == int(name[2]):
@@ -70,13 +69,7 @@ def tile_routed_moe_kernel(tc, xT, w1, w3, w2, gate, offs, pos1, pos2, out):
             else:
                 e = int(name[2])
                 raw, w = (w1_raw[e], w1) if name[1] == "1" else (w3_raw[e], w3)
-                if len(name) == 3:
-                    nc.sync.dma_start(out=raw[:], in_=w[e, :, :].rearrange("(p j) h -> p (j h)", j=J))
-                else:
-                    a = "ab".index(name[3])
-                    s = slice(a * (H // 2), (a + 1) * (H // 2))
-                    nc.sync.dma_start(out=raw[:].rearrange("p (j h) -> p j h", j=J)[:, :, s],
-                                      in_=w[e, :, :].rearrange("(p j) h -> p j h", j=J)[:, :, s])
+                nc.sync.dma_start(out=raw[:], in_=w[e, :, :].rearrange("(p j) h -> p (j h)", j=J))
 
         x_codes = held.tile([P, T], U32, name="x_codes", align_bytes=64)
         x_scales = held.tile([P, T], U8, name="x_scales", align_bytes=64)
@@ -86,11 +79,13 @@ def tile_routed_moe_kernel(tc, xT, w1, w3, w2, gate, offs, pos1, pos2, out):
             x_src = x_raw[h][:].rearrange("p j (c i) -> p c j i", i=4)
             x_dst = x_grouped[:, h * 1024:(h + 1) * 1024].rearrange("p (c i j) -> p c j i", i=4, j=J)
             cut = XV[h] // 4
-            if cut:
-                nc.vector.tensor_copy(out=x_dst[:, 0:cut], in_=x_src[:, 0:cut])
             if cut < 64:
                 nc.scalar.copy(out=x_dst[:, cut:64], in_=x_src[:, cut:64])
-        nc.vector.quantize_mx(out=x_codes[:].bitcast(FP8X4), scales=x_scales[:], in_=x_grouped[:])
+            if cut:
+                nc.vector.tensor_copy(out=x_dst[:, 0:cut], in_=x_src[:, 0:cut])
+            half = slice(h * (T // 2), (h + 1) * (T // 2))
+            nc.vector.quantize_mx(out=x_codes[:, half].bitcast(FP8X4), scales=x_scales[:, half],
+                                  in_=x_grouped[:, h * 1024:(h + 1) * 1024])
 
         s_codes = held.tile([P, SLOTS], U32, name="s_codes", align_bytes=64)
         s_scales = held.tile([P, SLOTS], U8, name="s_scales", align_bytes=64)
@@ -112,11 +107,8 @@ def tile_routed_moe_kernel(tc, xT, w1, w3, w2, gate, offs, pos1, pos2, out):
             if which == 0:
                 live["g", e] = stage.tile([P, 2, H * J], BF16, name="grouped", align_bytes=64)
             raw = (w1_raw, w3_raw)[which][e]
-            if which == 1 and e in S3:
-                parts = [(0, 64 - S3[e][0], 64), (64, 128 - S3[e][1], 128)]
-            else:
-                v = V1.get(e, 0) if which == 0 else 128
-                parts = [(0, v, 128)]
+            v = V1.get(e, 0) if which == 0 else 128 - S3.get(e, 0)
+            parts = [(0, v, 128)]
             for lo, cut, hi in parts:
                 if hi > cut:
                     src, dst = up_views(raw, live["g", e][:, which, :], cut, hi)
@@ -150,18 +142,24 @@ def tile_routed_moe_kernel(tc, xT, w1, w3, w2, gate, offs, pos1, pos2, out):
                 products(which, e)
 
         def silu(e):
-            sil = stage.tile([P, C, 4], F32, name="sil")
+            if e == E - 1:
+                sil = held.tile([P, C, 4], F32, name="sil_last", tag="last", align_bytes=64)
+            else:
+                sil = stage.tile([P, C, 4], F32, name="sil")
             nc.scalar.activation(sil[:], live["acc", 0, e][:].rearrange("p t c -> p c t"), SILU)
             live["sil", e] = sil
 
         def inter2(g):
-            grouped = held.tile([P, len(g), N * J], BF16, name=f"grp2_{g[0]}", align_bytes=64)
+            tag = "last" if g[-1] == E - 1 else f"grp2_{g[0]}"
+            grouped = held.tile([P, len(g), N * J], BF16, name=f"grp2_{g[0]}", tag=tag, align_bytes=64)
             src = w2_raw[g][:].rearrange("p e (j c i) -> p e c j i", j=J, i=4)
             dst = grouped[:].rearrange("p e (c i j) -> p e c j i", i=4, j=J)
-            if g in W2_ON_VECTOR:
-                nc.vector.tensor_copy(out=dst, in_=src)
-            else:
-                nc.scalar.copy(out=dst, in_=src)
+            on_vector = [e for e in g if e in W2_ON_VECTOR]
+            cut = on_vector[0] - g[0] if on_vector else len(g)
+            if cut:
+                nc.scalar.copy(out=dst[:, 0:cut], in_=src[:, 0:cut])
+            if cut < len(g):
+                nc.vector.tensor_copy(out=dst[:, cut:], in_=src[:, cut:])
             codes = held.tile([P, len(g), N], U32, name=f"cod2_{g[0]}", align_bytes=64)
             scales = held.tile([P, len(g), N], U8, name=f"scl2_{g[0]}", align_bytes=64)
             nc.vector.quantize_mx(
@@ -170,31 +168,41 @@ def tile_routed_moe_kernel(tc, xT, w1, w3, w2, gate, offs, pos1, pos2, out):
             for i, e in enumerate(g):
                 live["w2", e] = codes[:, i, :], scales[:, i, :]
 
+        h_group_of = {e: g for g in ((0, 1), (2, 3), (4, 5), (6,), (7,)) for e in g}
         group_of = {e: g for g in Y_GROUPS for e in g}
 
         def hid(e):
-            hb = stage.tile([P, C, 4], BF16, name="hb", align_bytes=64)
-            nc.vector.tensor_tensor(hb[:], live["acc", 1, e][:].rearrange("p t c -> p c t"), live["sil", e][:], MULT)
-            live["hb", e] = hb
+            grp = h_group_of[e]
+            if e == grp[0]:
+                live["hb", grp] = stage.tile([P, 2, C, 4], BF16, name="hb", align_bytes=64)
+            nc.vector.tensor_tensor(live["hb", grp][:, e - grp[0]], live["acc", 1, e][:].rearrange("p t c -> p c t"), live["sil", e][:], MULT)
 
-        def quanth(e):
-            codes = stage.tile([P, C], U32, name="codh", align_bytes=64)
-            scales = stage.tile([P, C], U8, name="sclh", align_bytes=64)
-            nc.vector.quantize_mx(out=codes[:].bitcast(FP8X4), scales=scales[:],
-                                  in_=live["hb", e][:].rearrange("p c t -> p (c t)"))
+        def quanth(grp):
+            n = len(grp)
+            codes = stage.tile([P, 2, C], U32, name="codh", align_bytes=64, bufs=E)
+            scales = stage.tile([P, 2, C], U8, name="sclh", align_bytes=64, bufs=E)
+            nc.vector.quantize_mx(out=codes[:, 0:n].rearrange("p e c -> p (e c)").bitcast(FP8X4),
+                                  scales=scales[:, 0:n].rearrange("p e c -> p (e c)"),
+                                  in_=live["hb", grp][:, 0:n].rearrange("p e c t -> p (e c t)"))
+            for i, e in enumerate(grp):
+                live["qh", e] = codes[:, i, :], scales[:, i, :]
+
+        def down(e):
+            codes, scales = live["qh", e]
             grp = group_of[e]
             if e == grp[0]:
                 live["y", grp] = psum.tile([P, 4, C], F32, name="acc_y", bufs=2)
             w2c, w2s = live["w2", e]
             nc.tensor.matmul_mx(
                 out=live["y", grp][:, e - grp[0], :], lhsT=w2c.bitcast(FP8X4), lhsT_scale=w2s,
-                rhs=codes[:].bitcast(FP8X4), rhs_scale=scales[:], start=True, stop=True)
+                rhs=codes.bitcast(FP8X4), rhs_scale=scales, start=True, stop=True)
 
         def fetch(grp):
             nc.scalar.copy(
                 out=y_sb[:, grp[0] * C:(grp[-1] + 1) * C].rearrange("p (g c) -> p g c", c=C),
                 in_=live["y", grp][:, 0:len(grp), :])
 
+        pending = []
         for e in range(E + 1):
             if e in GATHER_AT:
                 gather(*GATHERS[GATHER_AT[e]])
@@ -214,19 +222,25 @@ def tile_routed_moe_kernel(tc, xT, w1, w3, w2, gate, offs, pos1, pos2, out):
                 else:
                     quant((0, 1), e)
                     silu(e)
-            if e in W2_AT:
-                inter2(W2_AT[e])
             if e == E:
                 hid(e - 1)
             if e > 0:
-                quanth(e - 1)
-                if e - 1 == group_of[e - 1][-1]:
-                    fetch(group_of[e - 1])
+                if e - 1 == h_group_of[e - 1][-1]:
+                    quanth(h_group_of[e - 1])
+                    pending.extend(h_group_of[e - 1])
+            for g in W2_AT.get(e, ()):
+                inter2(g)
+            for d in list(pending):
+                if ("w2", d) in live:
+                    down(d)
+                    pending.remove(d)
+                    if d == group_of[d][-1]:
+                        fetch(group_of[d])
 
         r1 = held.tile([P, T], F32, name="r1")
         r2 = held.tile([P, T], F32, name="r2")
-        nc.vector.tensor_tensor(r1[:], y_sb[:].indirect(pos1_t[:]), gates[0][:], MULT)
-        nc.vector.tensor_tensor(r2[:], y_sb[:].indirect(pos2_t[:]), gates[1][:], MULT)
+        nc.vector.tensor_tensor(r1[:], y_sb[:].indirect(pos1_t[:]), gates[:, 0, :], MULT)
+        nc.vector.tensor_tensor(r2[:], y_sb[:].indirect(pos2_t[:]), gates[:, 1, :], MULT)
         res = held.tile([P, T], F32, name="res")
         for queue, toks in ((nc.sync, slice(0, T // 2)), (nc.scalar, slice(T // 2, T))):
             nc.vector.tensor_tensor(res[:, toks], r1[:, toks], r2[:, toks], ADD)

from contextlib import ExitStack

import concourse.mybir as mybir

K, T, E, C, H, N = 512, 512, 8, 128, 512, 128
SLOTS = E * C
FLOPS = 2 * SLOTS * (2 * K * H + H * N)

F32 = mybir.dt.float32
BF16 = mybir.dt.bfloat16
U32 = mybir.dt.uint32
U16 = mybir.dt.uint16
U8 = mybir.dt.uint8
FP8X4 = mybir.dt.float8_e4m3fn_x4
MULT = mybir.AluOpType.mult
ADD = mybir.AluOpType.add
SILU = mybir.ActivationFunctionType.Silu

P = 128
J = 4
LOADS = "offs xa xb w10 w30 w11 w31 pos w12 w32 w13 w33 w14 w34 w15 w35 w16 w36 w17 w37 w20 w24 w26 gate".split()
GATHERS = ((0, 2), (2, 3), (5, 3))
GATHER_AT = {0: 0, 1: 1, 3: 2}
Y_GROUPS = ((0, 1, 2, 3), (4, 5), (6, 7))
W2_GROUPS = ((0, 1, 2, 3), (4, 5), (6, 7))
W2_AT = {8: ((0, 1, 2, 3), (4, 5), (6, 7))}
W2_ON_VECTOR = (3, 5, 6, 7)
V1 = {7: 64}
S3 = {7: 48}
SEPARATE = (7,)
XV = (256, 256)


def tile_routed_moe_kernel(tc, xT, w1, w3, w2, gate, offs, pos1, pos2, out):
    nc = tc.nc
    with ExitStack() as ctx:
        held = ctx.enter_context(tc.tile_pool(name="held", bufs=1))
        stage = ctx.enter_context(tc.tile_pool(name="stage", bufs=2))
        psum = ctx.enter_context(tc.psum_pool(name="psum", bufs=3))

        offs_t = held.tile([P, SLOTS // 16], U16, name="offs_t")
        pos1_t = held.tile([P, T // 16], U16, name="pos1_t")
        pos2_t = held.tile([P, T // 16], U16, name="pos2_t")
        x_raw = [held.tile([P, J, T // 2], F32, name=f"x_raw{h}") for h in range(2)]
        gates = held.tile([P, 2, T], F32, name="gates")
        w1_raw = [held.tile([P, J * H], F32, name=f"w1_raw{e}") for e in range(E)]
        w3_raw = [held.tile([P, J * H], F32, name=f"w3_raw{e}") for e in range(E)]
        w2_raw = {g: held.tile([P, len(g), J * N], F32, name=f"w2_raw{g[0]}") for g in W2_GROUPS}

        warm = held.tile([P, 1], F32, name="warm")
        nc.vector.memset(warm[:], 0.0)
        nc.scalar.activation(warm[:], warm[:], SILU)

        for name in LOADS:
            if name == "offs":
                nc.sync.dma_start(offs_t[:], offs)
            elif name == "pos":
                nc.sync.dma_start(pos1_t[:], pos1)
                nc.sync.dma_start(pos2_t[:], pos2)
            elif name[0] == "x":
                h = "ab".index(name[1])
                nc.sync.dma_start(out=x_raw[h][:], in_=xT[:, h * (T // 2):(h + 1) * (T // 2)].rearrange("(p j) t -> p j t", j=J))
            elif name == "gate":
                nc.sync.dma_start(out=gates[:], in_=gate.rearrange("g p t -> p g t"))
            elif name[:2] == "w2":
                for g in W2_GROUPS:
                    if g[0] == int(name[2]):
                        nc.sync.dma_start(out=w2_raw[g][:], in_=w2[g[0]:g[-1] + 1, :, :].rearrange("e (p j) n -> p e (j n)", j=J))
            else:
                e = int(name[2])
                raw, w = (w1_raw[e], w1) if name[1] == "1" else (w3_raw[e], w3)
                nc.sync.dma_start(out=raw[:], in_=w[e, :, :].rearrange("(p j) h -> p (j h)", j=J))

        x_codes = held.tile([P, T], U32, name="x_codes", align_bytes=64)
        x_scales = held.tile([P, T], U8, name="x_scales", align_bytes=64)
        nc.gpsimd.memset(x_scales[:], 0)
        x_grouped = held.tile([P, T * J], BF16, name="x_grouped", align_bytes=64)
        for h in range(2):
            x_src = x_raw[h][:].rearrange("p j (c i) -> p c j i", i=4)
            x_dst = x_grouped[:, h * 1024:(h + 1) * 1024].rearrange("p (c i j) -> p c j i", i=4, j=J)
            cut = XV[h] // 4
            if cut < 64:
                nc.scalar.copy(out=x_dst[:, cut:64], in_=x_src[:, cut:64])
            if cut:
                nc.vector.tensor_copy(out=x_dst[:, 0:cut], in_=x_src[:, 0:cut])
            half = slice(h * (T // 2), (h + 1) * (T // 2))
            nc.vector.quantize_mx(out=x_codes[:, half].bitcast(FP8X4), scales=x_scales[:, half],
                                  in_=x_grouped[:, h * 1024:(h + 1) * 1024])

        s_codes = held.tile([P, SLOTS], U32, name="s_codes", align_bytes=64)
        s_scales = held.tile([P, SLOTS], U8, name="s_scales", align_bytes=64)
        y_sb = held.tile([P, SLOTS], F32, name="y_sb")
        live = {}

        def gather(first, count):
            cols = slice(first * C, (first + count) * C)
            lst = offs_t[:, first * C // 16:(first + count) * C // 16]
            nc.vector.tensor_copy(s_codes[:, cols], x_codes[:].indirect(lst))
            nc.vector.tensor_copy(s_scales[:, cols], x_scales[:].indirect(lst))

        def up_views(raw, grouped, m0, m1):
            src = raw[:].rearrange("p (j m t) -> p m j t", j=J, t=4)
            dst = grouped.rearrange("p (t m j) -> p m j t", t=4, j=J)
            return src[:, m0:m1], dst[:, m0:m1]

        def inter(which, e):
            if which == 0:
                live["g", e] = stage.tile([P, 2, H * J], BF16, name="grouped", align_bytes=64)
            raw = (w1_raw, w3_raw)[which][e]
            v = V1.get(e, 0) if which == 0 else 128 - S3.get(e, 0)
            parts = [(0, v, 128)]
            for lo, cut, hi in parts:
                if hi > cut:
                    src, dst = up_views(raw, live["g", e][:, which, :], cut, hi)
                    nc.scalar.copy(out=dst, in_=src)
                if cut > lo:
                    src, dst = up_views(raw, live["g", e][:, which, :], lo, cut)
                    nc.vector.tensor_copy(out=dst, in_=src)

        def products(which, e):
            codes, scales = live["q", e]
            acc = psum.tile([P, 4, C], F32, name=f"acc{which}", bufs=3)
            cols = slice(e * C, (e + 1) * C)
            for t in range(4):
                blk = slice(which * H + t * P, which * H + (t + 1) * P)
                nc.tensor.matmul_mx(
                    out=acc[:, t, :], lhsT=codes[:, blk].bitcast(FP8X4), lhsT_scale=scales[:, blk],
                    rhs=s_codes[:, cols].bitcast(FP8X4), rhs_scale=s_scales[:, cols], start=True, stop=True)
            live["acc", which, e] = acc

        def quant(whichs, e):
            if whichs[0] == 0:
                codes = stage.tile([P, 2 * H], U32, name="codes", align_bytes=64)
                scales = stage.tile([P, 2 * H], U8, name="scales", align_bytes=64)
                live["q", e] = codes, scales
            codes, scales = live["q", e]
            cols = slice(whichs[0] * H, (whichs[-1] + 1) * H)
            words = slice(whichs[0] * H * J, (whichs[-1] + 1) * H * J)
            nc.vector.quantize_mx(out=codes[:, cols].bitcast(FP8X4), scales=scales[:, cols],
                                  in_=live["g", e][:].rearrange("p w k -> p (w k)")[:, words])
            for which in whichs:
                products(which, e)

        def silu(e):
            if e == E - 1:
                sil = held.tile([P, C, 4], F32, name="sil_last", tag="last", align_bytes=64)
            else:
                sil = stage.tile([P, C, 4], F32, name="sil")
            nc.scalar.activation(sil[:], live["acc", 0, e][:].rearrange("p t c -> p c t"), SILU)
            live["sil", e] = sil

        def inter2(g):
            tag = "last" if g[-1] == E - 1 else f"grp2_{g[0]}"
            grouped = held.tile([P, len(g), N * J], BF16, name=f"grp2_{g[0]}", tag=tag, align_bytes=64)
            src = w2_raw[g][:].rearrange("p e (j c i) -> p e c j i", j=J, i=4)
            dst = grouped[:].rearrange("p e (c i j) -> p e c j i", i=4, j=J)
            on_vector = [e for e in g if e in W2_ON_VECTOR]
            cut = on_vector[0] - g[0] if on_vector else len(g)
            if cut:
                nc.scalar.copy(out=dst[:, 0:cut], in_=src[:, 0:cut])
            if cut < len(g):
                nc.vector.tensor_copy(out=dst[:, cut:], in_=src[:, cut:])
            codes = held.tile([P, len(g), N], U32, name=f"cod2_{g[0]}", align_bytes=64)
            scales = held.tile([P, len(g), N], U8, name=f"scl2_{g[0]}", align_bytes=64)
            nc.vector.quantize_mx(
                out=codes[:].rearrange("p e n -> p (e n)").bitcast(FP8X4),
                scales=scales[:].rearrange("p e n -> p (e n)"), in_=grouped[:].rearrange("p e n -> p (e n)"))
            for i, e in enumerate(g):
                live["w2", e] = codes[:, i, :], scales[:, i, :]

        h_group_of = {e: g for g in ((0, 1), (2, 3), (4, 5), (6,), (7,)) for e in g}
        group_of = {e: g for g in Y_GROUPS for e in g}

        def hid(e):
            grp = h_group_of[e]
            if e == grp[0]:
                live["hb", grp] = stage.tile([P, 2, C, 4], BF16, name="hb", align_bytes=64)
            nc.vector.tensor_tensor(live["hb", grp][:, e - grp[0]], live["acc", 1, e][:].rearrange("p t c -> p c t"), live["sil", e][:], MULT)

        def quanth(grp):
            n = len(grp)
            codes = stage.tile([P, 2, C], U32, name="codh", align_bytes=64, bufs=E)
            scales = stage.tile([P, 2, C], U8, name="sclh", align_bytes=64, bufs=E)
            nc.vector.quantize_mx(out=codes[:, 0:n].rearrange("p e c -> p (e c)").bitcast(FP8X4),
                                  scales=scales[:, 0:n].rearrange("p e c -> p (e c)"),
                                  in_=live["hb", grp][:, 0:n].rearrange("p e c t -> p (e c t)"))
            for i, e in enumerate(grp):
                live["qh", e] = codes[:, i, :], scales[:, i, :]

        def down(e):
            codes, scales = live["qh", e]
            grp = group_of[e]
            if e == grp[0]:
                live["y", grp] = psum.tile([P, 4, C], F32, name="acc_y", bufs=2)
            w2c, w2s = live["w2", e]
            nc.tensor.matmul_mx(
                out=live["y", grp][:, e - grp[0], :], lhsT=w2c.bitcast(FP8X4), lhsT_scale=w2s,
                rhs=codes.bitcast(FP8X4), rhs_scale=scales, start=True, stop=True)

        def fetch(grp):
            nc.scalar.copy(
                out=y_sb[:, grp[0] * C:(grp[-1] + 1) * C].rearrange("p (g c) -> p g c", c=C),
                in_=live["y", grp][:, 0:len(grp), :])

        pending = []
        for e in range(E + 1):
            if e in GATHER_AT:
                gather(*GATHERS[GATHER_AT[e]])
            if e < E:
                inter(0, e)
                if e in SEPARATE:
                    quant((0,), e)
                    silu(e)
                    if e > 0:
                        hid(e - 1)
                inter(1, e)
            if 0 < e < E and e not in SEPARATE:
                hid(e - 1)
            if e < E:
                if e in SEPARATE:
                    quant((1,), e)
                else:
                    quant((0, 1), e)
                    silu(e)
            if e == E:
                hid(e - 1)
            if e > 0:
                if e - 1 == h_group_of[e - 1][-1]:
                    quanth(h_group_of[e - 1])
                    pending.extend(h_group_of[e - 1])
            for g in W2_AT.get(e, ()):
                inter2(g)
            for d in list(pending):
                if ("w2", d) in live:
                    down(d)
                    pending.remove(d)
                    if d == group_of[d][-1]:
                        fetch(group_of[d])

        r1 = held.tile([P, T], F32, name="r1")
        r2 = held.tile([P, T], F32, name="r2")
        nc.vector.tensor_tensor(r1[:], y_sb[:].indirect(pos1_t[:]), gates[:, 0, :], MULT)
        nc.vector.tensor_tensor(r2[:], y_sb[:].indirect(pos2_t[:]), gates[:, 1, :], MULT)
        res = held.tile([P, T], F32, name="res")
        for queue, toks in ((nc.sync, slice(0, T // 2)), (nc.scalar, slice(T // 2, T))):
            nc.vector.tensor_tensor(res[:, toks], r1[:, toks], r2[:, toks], ADD)
            queue.dma_start(out=out[:, toks], in_=res[:, toks])
